import numpy as np
import ml_dtypes


def mxq(x, axis, fmt="e4m3"):
    dtype, down = {"e4m3": (ml_dtypes.float8_e4m3fn, 7), "e5m2": (ml_dtypes.float8_e5m2, 14)}[fmt]
    v = np.moveaxis(np.asarray(x, np.float32).astype(ml_dtypes.bfloat16).astype(np.float64), axis, -1)
    blocks = v.reshape(v.shape[:-1] + (-1, 32))
    amax = np.abs(blocks).max(-1, keepdims=True)
    byte = np.maximum(np.where(amax > 0, np.frexp(amax)[1] - 1 + 127, 0) - down, 1)
    scale = np.exp2(byte - 127.0)
    codes = (blocks / scale).astype(np.float32).astype(dtype).astype(np.float64)
    return np.moveaxis((codes * scale).reshape(v.shape), -1, axis)


WIDE = False


def mx_kscale(k):
    if not WIDE:
        return np.ones(k)
    levels = np.array([10, -10, 5, -5, 0])
    if k % 512:
        return np.exp2(np.random.permutation(np.resize(levels, k // 32))).repeat(32)
    a = np.empty((k // 512, 16))
    for p in range(k // 512):
        a[p, :8] = np.random.permutation(np.resize(levels, 8))
        for g in range(8):
            far = levels[np.abs(levels - a[p, g]) >= 10]
            a[p, g + 8] = far[np.random.randint(len(far))]
    return np.exp2(a.ravel()).repeat(32)


BF16 = ml_dtypes.bfloat16


def bf(x):
    return np.asarray(x, np.float32).astype(BF16)


def f64(x):
    return np.asarray(x).astype(np.float64)

def planes(Y):
    n, m = Y.shape
    b = f64(bf(Y)).reshape(n // 32, 32, m)
    amax = np.abs(b).max(1)
    byte = np.clip(np.where(amax > 0, np.frexp(amax)[1] - 1 + 127 - 7, 1), 1, 254)
    codes = (b * np.exp2(127.0 - byte)[:, None, :]).reshape(n, m).astype(np.float32).astype(ml_dtypes.float8_e4m3fn).view(np.uint8)
    words = codes.reshape(n // 512, 128, 4, m).transpose(0, 1, 3, 2)
    return np.ascontiguousarray(words), np.ascontiguousarray(byte.astype(np.uint8).reshape(n // 512, 16, m))


B, G, F, O = 1024, 2048, 512, 32
CX = 0.75 * (3.0 / np.pi) ** (1.0 / 3.0)

def setup_inputs():
    s = mx_kscale(B)
    t = mx_kscale(B)
    c = np.random.randn(O, B) * (O * B) ** -0.25
    dens = sum(v[:, None] * v[None, :] for v in c)
    chi = np.random.randn(B, G)
    frag = np.exp(0.5 * np.random.randn(B, F)) / np.sqrt(O * B)
    core = 0.1 + 0.3 * np.abs(np.random.randn(G, F))
    wx = -CX * np.exp(0.8 * np.random.randn(G))
    return {
        "chi": bf(chi * s[:, None]),
        "dens": bf(dens * (t / s)[:, None] / s[None, :]),
        "frag": bf(frag / t[:, None]),
        "core": bf(core),
        "wx": bf(wx),
    }

def reference(chi, dens, frag, core, wx):
    chi, dens, frag, core, wx = f64(chi), f64(dens), f64(frag), f64(core), f64(wx)
    T = mxq(dens, 1, "e4m3") @ mxq(chi, 0, "e4m3")
    H = T * chi
    rho = (mxq(H, 0, "e4m3").T @ mxq(frag, 0, "e4m3")) + core
    y = rho ** (1.0 / 3.0) * rho * wx[:, None]
    Y = y.reshape(G, F)
    words, scales = planes(Y)
    return y, words, scales

@@ -1,0 +1,398 @@
+from contextlib import ExitStack
+
+import concourse.mybir as mybir
+from concourse.masks import make_identity
+
+B, G, F = 1024, 2048, 512
+FLOPS = 2 * B * B * G + 2 * G * B * F
+
+F32 = mybir.dt.float32
+BF16 = mybir.dt.bfloat16
+U32 = mybir.dt.uint32
+I32 = mybir.dt.int32
+U8 = mybir.dt.uint8
+FP8X4 = mybir.dt.float8_e4m3fn_x4
+ALU = mybir.AluOpType
+ACT = mybir.ActivationFunctionType
+
+P = 128
+PACK = 4
+SPAN = P * PACK
+HALVES = B // SPAN
+SLABS = G // SPAN
+NT = 4
+
+
+def tile_fragment_lda_exchange_h3_kernel(tc, chi, dens, frag, core, wx, out_0, out_1, out_2):
+    nc = tc.nc
+    V, S, GP = nc.vector, nc.scalar, nc.gpsimd
+    with ExitStack() as ctx:
+        sb = ctx.enter_context(tc.tile_pool(name="sb", bufs=1))
+        ps = ctx.enter_context(tc.psum_pool(name="ps", bufs=1))
+
+        def tiles(name, count, shape, dtype):
+            return [sb.tile(shape, dtype, name="%s%d" % (name, i), align_bytes=64) for i in range(count)]
+
+        banks = [ps.tile([P, SPAN], F32, name="bank%d" % i) for i in range(8)]
+        t_banks, rho_banks = banks[:NT], banks[NT:]
+
+        ident = sb.tile([P, P], F32, name="ident")
+        warm = sb.tile([P, 8], F32, name="warm")
+        dens_raw = tiles("dens_raw", 4, [P, 2, B], BF16)
+        dens_words = tiles("dens_words", 2, [P, 2, HALVES, P, 2], F32)
+        dens_codes = tiles("dens_codes", HALVES, [P, PACK, HALVES, P], U32)
+        dens_scales = tiles("dens_scales", HALVES, [P, PACK, HALVES, P], U8)
+        chi_raw = tiles("chi_raw", SLABS * HALVES, [P, PACK, SPAN], BF16)
+        h_pairs = tiles("h_pairs", SLABS, [P, HALVES, SPAN * PACK], BF16)
+        chi_mixed = [t[:] for t in tiles("chi_mixed", (SLABS - 1) * HALVES - 1, [P, SPAN, PACK], BF16)]
+        chi_mixed = chi_mixed[:3] + [dens_words[1][:].rearrange("p t k m u -> p (t k m u)").bitcast(BF16).rearrange("p (c j) -> p c j", j=PACK)] + chi_mixed[3:]
+        frag_mixed = tiles("frag_mixed", HALVES, [P, F, PACK], BF16)
+        chi_mixed += [h_pairs[0][:, 0, :].rearrange("p (c j) -> p c j", j=PACK), frag_mixed[1][:]]
+        chi_codes = tiles("chi_codes", 2 * HALVES, [P, SPAN], U32)
+        chi_scales = tiles("chi_scales", 2 * HALVES, [P, SPAN], U8)
+        frag_raw = tiles("frag_raw", HALVES, [P, PACK, F], BF16)
+        frag_codes = tiles("frag_codes", HALVES, [P, F], U32)
+        frag_scales = tiles("frag_scales", HALVES, [P, F], U8)
+        h_codes = sb.tile([P, HALVES * SPAN], U32, name="h_codes", align_bytes=64)
+        h_scales = sb.tile([P, HALVES * SPAN], U8, name="h_scales", align_bytes=64)
+        core_sb = tiles("core_sb", SLABS, [P, PACK, F], BF16)
+        wx_sb = sb.tile([P, SLABS, PACK], BF16, name="wx_sb")
+        wx_f32 = sb.tile([P, SLABS, PACK], F32, name="wx_f32")
+        rho = 2 * tiles("rho", 2, [P, PACK, F], F32)
+        y = [
+            h_pairs[slab + 1][:].rearrange("p h c -> p (h c)").bitcast(F32).rearrange("p (s f) -> p s f", s=PACK)
+            for slab in range(SLABS - 1)
+        ] + [rho[3][:]]
+        y_mixed = tiles("y_mixed", 2, [P, F, PACK], BF16)
+        y_codes = tiles("y_codes", SLABS, [P, F], U32)
+        y_scales = sb.tile([P, SLABS, F], U8, name="y_scales", align_bytes=64)
+
+        def rows4(matrix, span):
+            return matrix[span * SPAN : (span + 1) * SPAN, :].rearrange("(p j) w -> p j w", j=PACK)
+
+        def copy_on(engine, out, in_):
+            if engine is S:
+                engine.copy(out=out, in_=in_)
+            elif engine is V:
+                engine.tensor_copy(out=out, in_=in_)
+            else:
+                engine.tensor_scalar(out=out, in0=in_, scalar1=1.0, scalar2=0.0, op0=ALU.mult, op1=ALU.add)
+
+        def interleave(engine, mixed, raw, lo, hi):
+            if engine is GP:
+                copy_on(engine, mixed[:, lo:hi, :], raw[:, :, lo:hi].rearrange("p j c -> p c j"))
+            else:
+                copy_on(
+                    engine,
+                    mixed[:, lo:hi, :].rearrange("p (c i) j -> p c j i", i=4),
+                    raw[:, :, lo:hi].rearrange("p j (c i) -> p c j i", i=4),
+                )
+
+        def quantize(codes, scales, values):
+            nc.vector.quantize_mx(out=codes.bitcast(FP8X4), scales=scales, in_=values)
+
+        def load_dens(half, pair):
+            nc.sync.dma_start(out=dens_raw[2 * half + pair][:], in_=rows4(dens, half)[:, 2 * pair : 2 * pair + 2, :])
+
+        def load_chi(slab, half):
+            nc.sync.dma_start(
+                out=chi_raw[2 * slab + half][:], in_=rows4(chi, half)[:, :, slab * SPAN : (slab + 1) * SPAN]
+            )
+
+        def load_frag(half):
+            nc.sync.dma_start(out=frag_raw[half][:], in_=rows4(frag, half))
+
+        def load_core(slab):
+            nc.sync.dma_start(out=core_sb[slab][:], in_=rows4(core, slab))
+
+        def load_wx():
+            nc.sync.dma_start(out=wx_sb[:], in_=wx.rearrange("(g p s) -> p g s", p=P, s=PACK))
+
+        def widen_wx():
+            nc.scalar.copy(out=wx_f32[:], in_=wx_sb[:])
+
+        def dens_bank(pair, tt):
+            return banks[8 - 4 + 2 * pair + tt][:].rearrange("p (k u m) -> p k u m", k=HALVES, u=2)
+
+        def turn_dens(half, pair):
+            words = dens_raw[2 * half + pair][:].bitcast(F32)
+            for tt in range(2):
+                for k in range(HALVES):
+                    for u in range(2):
+                        nc.tensor.transpose(
+                            dens_bank(pair, tt)[:, k, u, :], words[:, tt, 256 * k + u : 256 * (k + 1) : 2], ident[:]
+                        )
+
+        def drain_dens(engine, pair, tt):
+            copy_on(engine, dens_words[pair][:, tt, :, :, :], dens_bank(pair, tt).rearrange("p k u m -> p k m u"))
+
+        def quantize_dens(half, pair):
+            ts = slice(2 * pair, 2 * pair + 2)
+            quantize(
+                dens_codes[half][:, ts, :, :].rearrange("p t k m -> p (t k m)"),
+                dens_scales[half][:, ts, :, :].rearrange("p t k m -> p (t k m)"),
+                dens_words[pair][:].rearrange("p t k m u -> p (t k m u)").bitcast(BF16),
+            )
+
+        def mix_chi(engine, slab, half, lo=0, hi=SPAN):
+            interleave(engine, chi_mixed[2 * slab + half], chi_raw[2 * slab + half], lo, hi)
+
+        def quantize_chi(slab, half, lo=0, hi=SPAN):
+            i = 2 * (slab % 2) + half
+            quantize(
+                chi_codes[i][:, lo:hi],
+                chi_scales[i][:, lo:hi],
+                chi_mixed[2 * slab + half][:, lo:hi, :].rearrange("p c j -> p (c j)"),
+            )
+
+        def mix_frag(engine, half, lo=0, hi=F):
+            interleave(engine, frag_mixed[half], frag_raw[half], lo, hi)
+
+        def quantize_frag(half):
+            quantize(frag_codes[half][:], frag_scales[half][:], frag_mixed[half][:].rearrange("p c j -> p (c j)"))
+
+        def t_bank(slab, half, c):
+            return t_banks[(8 * slab + 4 * half + c) % NT]
+
+        def first_product(slab, half, c):
+            cols = slice(c * P, (c + 1) * P)
+            for t in range(PACK):
+                for k in range(HALVES):
+                    i = 2 * (slab % 2) + k
+                    nc.tensor.matmul_mx(
+                        out=t_bank(slab, half, c)[:, t * P : (t + 1) * P],
+                        lhsT=dens_codes[half][:, t, k, :].bitcast(FP8X4),
+                        lhsT_scale=dens_scales[half][:, t, k, :],
+                        rhs=chi_codes[i][:, cols].bitcast(FP8X4),
+                        rhs_scale=chi_scales[i][:, cols],
+                        start=(k == 0),
+                        stop=(k == HALVES - 1),
+                    )
+
+        def times_chi(slab, half, c):
+            nc.vector.tensor_tensor(
+                out=h_pairs[slab][:].rearrange("p x (y h m t) -> p (x y) h m t", y=2, h=HALVES, t=PACK)[
+                    :, :, half, 32 * c : 32 * (c + 1), :
+                ],
+                in0=t_bank(slab, half, c)[:].rearrange("p (t m s) -> p s m t", t=PACK, s=PACK),
+                in1=chi_mixed[2 * slab + half][:, c * P : (c + 1) * P, :].rearrange("p (m s) t -> p s m t", s=PACK),
+                op=ALU.mult,
+            )
+
+        def quantize_h(slab, s):
+            lo, hi = s * HALVES * P, (s + 1) * HALVES * P
+            quantize(
+                h_codes[:, lo:hi], h_scales[:, lo:hi], h_pairs[slab][:].rearrange("p x c -> p (x c)")[:, PACK * lo : PACK * hi]
+            )
+
+        def rho_bank(slab, s):
+            return rho_banks[(4 * slab + s) % (8 - NT)]
+
+        def second_product(slab, s):
+            for half in range(HALVES):
+                cols = slice((HALVES * s + half) * P, (HALVES * s + half + 1) * P)
+                nc.tensor.matmul_mx(
+                    out=rho_bank(slab, s)[:],
+                    lhsT=h_codes[:, cols].bitcast(FP8X4),
+                    lhsT_scale=h_scales[:, cols],
+                    rhs=frag_codes[half][:].bitcast(FP8X4),
+                    rhs_scale=frag_scales[half][:],
+                    start=(half == 0),
+                    stop=(half == HALVES - 1),
+                )
+
+        def add_core(slab, s):
+            nc.vector.tensor_tensor(out=rho[slab][:, s, :], in0=rho_bank(slab, s)[:], in1=core_sb[slab][:, s, :], op=ALU.add)
+
+        def log_rho(slab, s0=0, s1=PACK):
+            nc.scalar.activation(out=rho[slab][:, s0:s1, :], in_=rho[slab][:, s0:s1, :], func=ACT.Ln)
+
+        def power(slab, s0=0, s1=PACK, lo=0, hi=F):
+            nc.scalar.activation(out=rho[slab][:, s0:s1, lo:hi], in_=rho[slab][:, s0:s1, lo:hi], func=ACT.Exp, scale=4.0 / 3.0)
+
+        def weigh(engine, slab, s, lo=0, hi=F):
+            piece, src, w = y[slab][:, s, lo:hi], rho[slab][:, s, lo:hi], wx_f32[:, slab, s : s + 1]
+            if engine is S:
+                engine.activation(out=piece, in_=src, func=ACT.Copy, scale=w)
+            else:
+                engine.tensor_scalar(out=piece, in0=src, scalar1=w, scalar2=0.0, op0=ALU.mult, op1=ALU.add)
+
+        def mix_y(engine, slab, lo=0, hi=F):
+            interleave(engine, y_mixed[slab % 2], y[slab], lo, hi)
+
+        def quantize_y(slab, lo=0, hi=F):
+            quantize(
+                y_codes[slab][:, lo:hi],
+                y_scales[:, slab, lo:hi],
+                y_mixed[slab % 2][:, lo:hi, :].rearrange("p c j -> p (c j)"),
+            )
+
+        def store_y(slab, lo=0, hi=F, queue=nc.sync):
+            queue.dma_start(out=rows4(out_0, slab)[:, :, lo:hi], in_=y[slab][:, :, lo:hi])
+
+        def store_codes(slab, lo=0, hi=F, queue=nc.sync):
+            queue.dma_start(
+                out=out_1[slab, :, lo:hi, :].rearrange("p m t -> p (m t)").bitcast(I32),
+                in_=y_codes[slab][:, lo:hi].bitcast(I32),
+            )
+
+        def store_scales(q, lo, hi, queue=nc.sync):
+            queue.dma_start(
+                out=out_2[lo:hi, 4 * q : 4 * q + 4, :].rearrange("g r m -> r g m").bitcast(I32),
+                in_=y_scales[32 * q : 32 * q + 4, lo:hi, :].bitcast(I32),
+            )
+
+        with tc.manual_schedule():
+            load_dens(0, 0)
+            load_dens(0, 1)
+            load_chi(0, 0)
+            load_chi(0, 1)
+            load_dens(1, 0)
+            load_dens(1, 1)
+            load_chi(1, 0)
+            load_chi(1, 1)
+            load_frag(0)
+            load_frag(1)
+            load_chi(2, 0)
+            load_chi(3, 1)
+            load_core(0)
+            load_chi(2, 1)
+            load_chi(3, 0)
+            load_wx()
+            load_core(1)
+            load_core(2)
+            load_core(3)
+            make_identity(nc, ident[:])
+            V.memset(warm[:], 1.0)
+            S.activation(out=warm[:], in_=warm[:], func=ACT.Ln)
+
+            turn_dens(0, 0)
+            turn_dens(0, 1)
+            drain_dens(S, 0, 0)
+            drain_dens(V, 0, 1)
+            drain_dens(S, 1, 0)
+            drain_dens(S, 1, 1)
+            mix_chi(V, 0, 0, 0, 256)
+            quantize_dens(0, 0)
+            quantize_chi(0, 0, 0, 256)
+            mix_chi(V, 0, 1, 0, 256)
+            quantize_dens(0, 1)
+            quantize_chi(0, 1, 0, 256)
+            mix_chi(S, 0, 0, 256, 512)
+            mix_chi(S, 0, 1, 256, 512)
+            turn_dens(1, 0)
+            first_product(0, 0, 0)
+            first_product(0, 0, 1)
+            quantize_chi(0, 0, 256, 512)
+            drain_dens(S, 0, 0)
+            drain_dens(S, 0, 1)
+            turn_dens(1, 1)
+            quantize_chi(0, 1, 256, 512)
+            first_product(0, 0, 2)
+            first_product(0, 0, 3)
+            drain_dens(S, 1, 0)
+            drain_dens(S, 1, 1)
+            times_chi(0, 0, 0)
+            quantize_dens(1, 0)
+            times_chi(0, 0, 1)
+            quantize_dens(1, 1)
+            mix_chi(GP, 1, 1)
+            times_chi(0, 0, 2)
+            times_chi(0, 0, 3)
+            mix_chi(S, 1, 0)
+            mix_frag(S, 0)
+            mix_frag(S, 1)
+            mix_chi(S, 2, 0)
+            mix_chi(S, 2, 1)
+            for c in range(4):
+                first_product(0, 1, c)
+                times_chi(0, 1, c)
+            for slab in range(1, SLABS):
+                if slab < 3:
+                    quantize_chi(slab, 0)
+                    quantize_chi(slab, 1)
+                    for c in range(3):
+                        first_product(slab, 0, c)
+                if slab == 1:
+                    quantize_frag(0)
+                if slab == 2:
+                    quantize_chi(3, 0)
+                    quantize_chi(3, 1)
+                if slab == 3:
+                    times_chi(slab, 0, 0)
+                for s in range(PACK):
+                    quantize_h(slab - 1, s)
+                if slab < 3:
+                    times_chi(slab, 0, 0)
+                if slab == 1:
+                    times_chi(slab, 0, 1)
+                    quantize_frag(1)
+                    mix_chi(GP, 3, 1)
+                    mix_chi(GP, 3, 0)
+                    widen_wx()
+                else:
+                    for s in (3, 2, 1, 0):
+                        weigh(GP, slab - 2, s)
+                    store_y(slab - 2)
+                    mix_y(GP, slab - 2)
+                if slab == 1:
+                    first_product(slab, 0, 3)
+                for s in range(PACK):
+                    second_product(slab - 1, s)
+                if slab == 1:
+                    times_chi(slab, 0, 2)
+                    times_chi(slab, 0, 3)
+                if slab == 2:
+                    first_product(slab, 0, 3)
+                    times_chi(slab, 0, 1)
+                for s in range(PACK):
+                    add_core(slab - 1, s)
+                    log_rho(slab - 1, s, s + 1)
+                for s in (3, 2, 1, 0):
+                    power(slab - 1, s, s + 1)
+                if slab > 1:
+                    for c in range(4 - slab, 4):
+                        times_chi(slab, 0, c)
+                for c in range(4):
+                    first_product(slab, 1, c)
+                for c in range(4):
+                    times_chi(slab, 1, c)
+                    if slab == 2:
+                        first_product(3, 0, c)
+            quantize_y(0)
+            store_codes(0)
+            for s in range(PACK):
+                quantize_h(3, s)
+                second_product(3, s)
+            for s in (3, 2, 1, 0):
+                weigh(GP, 2, s)
+            store_y(2)
+            for s in range(PACK):
+                add_core(3, s)
+                log_rho(3, s, s + 1)
+            quantize_y(1)
+            store_codes(1)
+            mix_y(V, 2)
+            for lo in range(0, F, 128):
+                power(3, 0, PACK, lo, lo + 128)
+            quantize_y(2)
+            store_codes(2)
+            for q in range(4):
+                store_scales(q, 0, 3)
+            for lo in range(0, F, 128):
+                for s in range(PACK):
+                    weigh(V, 3, s, lo, lo + 128)
+                if lo % 256:
+                    store_y(3, lo - 128, lo + 128)
+                if lo == 128:
+                    mix_y(V, 3, 0, 128)
+                if lo == 256:
+                    mix_y(V, 3, 128, 256)
+                    mix_y(S, 3, 256, 384)
+            quantize_y(3, 0, 256)
+            store_codes(3, 0, 256, queue=S)
+            mix_y(V, 3, 384, 512)
+            quantize_y(3, 256, 512)
+            store_codes(3, 256, 512, queue=S)
+            for q in range(4):
+                store_scales(q, 3, 4, S if q % 2 else nc.sync)

@@ -20,7 +20,6 @@ PACK = 4
 SPAN = P * PACK
 HALVES = B // SPAN
 SLABS = G // SPAN
-NT = 4
 
 
 def tile_fragment_lda_exchange_h3_kernel(tc, chi, dens, frag, core, wx, out_0, out_1, out_2):
@@ -34,18 +33,22 @@ def tile_fragment_lda_exchange_h3_kernel(tc, chi, dens, frag, core, wx, out_0, o
             return [sb.tile(shape, dtype, name="%s%d" % (name, i), align_bytes=64) for i in range(count)]
 
         banks = [ps.tile([P, SPAN], F32, name="bank%d" % i) for i in range(8)]
-        t_banks, rho_banks = banks[:NT], banks[NT:]
+        t_banks, rho_banks = banks[:4], banks[4:]
 
         ident = sb.tile([P, P], F32, name="ident")
         warm = sb.tile([P, 8], F32, name="warm")
         dens_raw = tiles("dens_raw", 4, [P, 2, B], BF16)
-        dens_words = tiles("dens_words", 2, [P, 2, HALVES, P, 2], F32)
+        dens_words = tiles("dens_words", 4, [P, 2, HALVES, P, 2], F32)
         dens_codes = tiles("dens_codes", HALVES, [P, PACK, HALVES, P], U32)
         dens_scales = tiles("dens_scales", HALVES, [P, PACK, HALVES, P], U8)
         chi_raw = tiles("chi_raw", SLABS * HALVES, [P, PACK, SPAN], BF16)
         h_pairs = tiles("h_pairs", SLABS, [P, HALVES, SPAN * PACK], BF16)
-        chi_mixed = [t[:] for t in tiles("chi_mixed", (SLABS - 1) * HALVES - 1, [P, SPAN, PACK], BF16)]
-        chi_mixed = chi_mixed[:3] + [dens_words[1][:].rearrange("p t k m u -> p (t k m u)").bitcast(BF16).rearrange("p (c j) -> p c j", j=PACK)] + chi_mixed[3:]
+        chi_shared = sb.tile([P, SPAN + SPAN // 2, PACK], BF16, name="chi_shared", align_bytes=64)
+        own = tiles("chi_mixed", 4, [P, SPAN, PACK], BF16)
+        chi_mixed = [chi_shared[:, SPAN // 2 :, :], own[0][:], own[1][:], chi_shared[:, :SPAN, :], own[2][:], own[3][:]]
+        ones = sb.tile([P, SPAN], BF16, name="ones", align_bytes=64)
+        ones_codes = sb.tile([P, P], U32, name="ones_codes", align_bytes=64)
+        ones_scales = sb.tile([P, P], U8, name="ones_scales", align_bytes=64)
         frag_mixed = tiles("frag_mixed", HALVES, [P, F, PACK], BF16)
         chi_mixed += [h_pairs[0][:, 0, :].rearrange("p (c j) -> p c j", j=PACK), frag_mixed[1][:]]
         chi_codes = tiles("chi_codes", 2 * HALVES, [P, SPAN], U32)
@@ -94,9 +97,10 @@ def tile_fragment_lda_exchange_h3_kernel(tc, chi, dens, frag, core, wx, out_0, o
         def load_dens(half, pair):
             nc.sync.dma_start(out=dens_raw[2 * half + pair][:], in_=rows4(dens, half)[:, 2 * pair : 2 * pair + 2, :])
 
-        def load_chi(slab, half):
+        def load_chi(slab, half, lo=0, hi=SPAN):
             nc.sync.dma_start(
-                out=chi_raw[2 * slab + half][:], in_=rows4(chi, half)[:, :, slab * SPAN : (slab + 1) * SPAN]
+                out=chi_raw[2 * slab + half][:, :, lo:hi],
+                in_=rows4(chi, half)[:, :, slab * SPAN + lo : slab * SPAN + hi],
             )
 
         def load_frag(half):
@@ -111,8 +115,8 @@ def tile_fragment_lda_exchange_h3_kernel(tc, chi, dens, frag, core, wx, out_0, o
         def widen_wx():
             nc.scalar.copy(out=wx_f32[:], in_=wx_sb[:])
 
-        def dens_bank(pair, tt):
-            return banks[8 - 4 + 2 * pair + tt][:].rearrange("p (k u m) -> p k u m", k=HALVES, u=2)
+        def dens_bank(half, pair, tt):
+            return banks[4 * (1 - half) + 2 * pair + tt][:].rearrange("p (k u m) -> p k u m", k=HALVES, u=2)
 
         def turn_dens(half, pair):
             words = dens_raw[2 * half + pair][:].bitcast(F32)
@@ -120,18 +124,22 @@ def tile_fragment_lda_exchange_h3_kernel(tc, chi, dens, frag, core, wx, out_0, o
                 for k in range(HALVES):
                     for u in range(2):
                         nc.tensor.transpose(
-                            dens_bank(pair, tt)[:, k, u, :], words[:, tt, 256 * k + u : 256 * (k + 1) : 2], ident[:]
+                            dens_bank(half, pair, tt)[:, k, u, :], words[:, tt, 256 * k + u : 256 * (k + 1) : 2], ident[:]
                         )
 
-        def drain_dens(engine, pair, tt):
-            copy_on(engine, dens_words[pair][:, tt, :, :, :], dens_bank(pair, tt).rearrange("p k u m -> p k m u"))
+        def drain_dens(engine, half, pair, tt):
+            copy_on(
+                engine,
+                dens_words[2 * half + pair][:, tt, :, :, :],
+                dens_bank(half, pair, tt).rearrange("p k u m -> p k m u"),
+            )
 
         def quantize_dens(half, pair):
             ts = slice(2 * pair, 2 * pair + 2)
             quantize(
                 dens_codes[half][:, ts, :, :].rearrange("p t k m -> p (t k m)"),
                 dens_scales[half][:, ts, :, :].rearrange("p t k m -> p (t k m)"),
-                dens_words[pair][:].rearrange("p t k m u -> p (t k m u)").bitcast(BF16),
+                dens_words[2 * half + pair][:].rearrange("p t k m u -> p (t k m u)").bitcast(BF16),
             )
 
         def mix_chi(engine, slab, half, lo=0, hi=SPAN):
@@ -152,7 +160,9 @@ def tile_fragment_lda_exchange_h3_kernel(tc, chi, dens, frag, core, wx, out_0, o
             quantize(frag_codes[half][:], frag_scales[half][:], frag_mixed[half][:].rearrange("p c j -> p (c j)"))
 
         def t_bank(slab, half, c):
-            return t_banks[(8 * slab + 4 * half + c) % NT]
+            if slab == 0:
+                return t_banks[2 * half + c % 2]
+            return t_banks[c]
 
         def first_product(slab, half, c):
             cols = slice(c * P, (c + 1) * P)
@@ -168,6 +178,19 @@ def tile_fragment_lda_exchange_h3_kernel(tc, chi, dens, frag, core, wx, out_0, o
                         start=(k == 0),
                         stop=(k == HALVES - 1),
                     )
+
+        def keep_warm(bank, passes=8):
+            codes, scales = ones_codes, ones_scales
+            for i in range(passes):
+                nc.tensor.matmul_mx(
+                    out=bank[:, :P],
+                    lhsT=codes[:, :P].bitcast(FP8X4),
+                    lhsT_scale=scales[:, :P],
+                    rhs=codes[:, :P].bitcast(FP8X4),
+                    rhs_scale=scales[:, :P],
+                    start=True,
+                    stop=True,
+                )
 
         def times_chi(slab, half, c):
             nc.vector.tensor_tensor(
@@ -186,7 +209,7 @@ def tile_fragment_lda_exchange_h3_kernel(tc, chi, dens, frag, core, wx, out_0, o
             )
 
         def rho_bank(slab, s):
-            return rho_banks[(4 * slab + s) % (8 - NT)]
+            return rho_banks[(4 * slab + s) % 4]
 
         def second_product(slab, s):
             for half in range(HALVES):
@@ -201,11 +224,13 @@ def tile_fragment_lda_exchange_h3_kernel(tc, chi, dens, frag, core, wx, out_0, o
                     stop=(half == HALVES - 1),
                 )
 
-        def add_core(slab, s):
-            nc.vector.tensor_tensor(out=rho[slab][:, s, :], in0=rho_bank(slab, s)[:], in1=core_sb[slab][:, s, :], op=ALU.add)
+        def add_core(slab, s, lo=0, hi=F):
+            nc.vector.tensor_tensor(
+                out=rho[slab][:, s, lo:hi], in0=rho_bank(slab, s)[:, lo:hi], in1=core_sb[slab][:, s, lo:hi], op=ALU.add
+            )
 
-        def log_rho(slab, s0=0, s1=PACK):
-            nc.scalar.activation(out=rho[slab][:, s0:s1, :], in_=rho[slab][:, s0:s1, :], func=ACT.Ln)
+        def log_rho(slab, s, lo=0, hi=F):
+            nc.scalar.activation(out=rho[slab][:, s, lo:hi], in_=rho[slab][:, s, lo:hi], func=ACT.Ln)
 
         def power(slab, s0=0, s1=PACK, lo=0, hi=F):
             nc.scalar.activation(out=rho[slab][:, s0:s1, lo:hi], in_=rho[slab][:, s0:s1, lo:hi], func=ACT.Exp, scale=4.0 / 3.0)
@@ -245,10 +270,12 @@ def tile_fragment_lda_exchange_h3_kernel(tc, chi, dens, frag, core, wx, out_0, o
         with tc.manual_schedule():
             load_dens(0, 0)
             load_dens(0, 1)
-            load_chi(0, 0)
-            load_chi(0, 1)
             load_dens(1, 0)
             load_dens(1, 1)
+            load_chi(0, 0, 0, 256)
+            load_chi(0, 1, 0, 256)
+            load_chi(0, 0, 256, 512)
+            load_chi(0, 1, 256, 512)
             load_chi(1, 0)
             load_chi(1, 1)
             load_frag(0)
@@ -262,51 +289,52 @@ def tile_fragment_lda_exchange_h3_kernel(tc, chi, dens, frag, core, wx, out_0, o
             load_core(1)
             load_core(2)
             load_core(3)
+            V.memset(ones[:], 1.0)
+            quantize(ones_codes[:], ones_scales[:], ones[:])
+            keep_warm(banks[0], 16)
             make_identity(nc, ident[:])
-            V.memset(warm[:], 1.0)
-            S.activation(out=warm[:], in_=warm[:], func=ACT.Ln)
-
-            turn_dens(0, 0)
-            turn_dens(0, 1)
-            drain_dens(S, 0, 0)
-            drain_dens(V, 0, 1)
-            drain_dens(S, 1, 0)
-            drain_dens(S, 1, 1)
-            mix_chi(V, 0, 0, 0, 256)
+            S.activation(out=warm[:], in_=ones[:, :8], func=ACT.Ln)
+            for half in range(2):
+                for pair in range(2):
+                    if (half, pair) == (1, 0):
+                        keep_warm(banks[3])
+                    turn_dens(half, pair)
+                    drain_dens(S, half, pair, 0)
+                    drain_dens(V if (half, pair) == (0, 0) else S, half, pair, 1)
             quantize_dens(0, 0)
-            quantize_chi(0, 0, 0, 256)
-            mix_chi(V, 0, 1, 0, 256)
             quantize_dens(0, 1)
+            keep_warm(banks[4])
+            mix_chi(V, 0, 0, 0, 256)
+            mix_chi(V, 0, 1, 0, 256)
+            quantize_chi(0, 0, 0, 256)
             quantize_chi(0, 1, 0, 256)
-            mix_chi(S, 0, 0, 256, 512)
+            quantize_dens(1, 0)
+            quantize_dens(1, 1)
+            mix_chi(V, 0, 0, 256, 512)
             mix_chi(S, 0, 1, 256, 512)
-            turn_dens(1, 0)
             first_product(0, 0, 0)
             first_product(0, 0, 1)
-            quantize_chi(0, 0, 256, 512)
-            drain_dens(S, 0, 0)
-            drain_dens(S, 0, 1)
-            turn_dens(1, 1)
-            quantize_chi(0, 1, 256, 512)
-            first_product(0, 0, 2)
-            first_product(0, 0, 3)
-            drain_dens(S, 1, 0)
-            drain_dens(S, 1, 1)
+            first_product(0, 1, 0)
+            first_product(0, 1, 1)
             times_chi(0, 0, 0)
-            quantize_dens(1, 0)
+            quantize_chi(0, 0, 256, 512)
+            quantize_chi(0, 1, 256, 512)
             times_chi(0, 0, 1)
-            quantize_dens(1, 1)
             mix_chi(GP, 1, 1)
-            times_chi(0, 0, 2)
-            times_chi(0, 0, 3)
             mix_chi(S, 1, 0)
             mix_frag(S, 0)
             mix_frag(S, 1)
             mix_chi(S, 2, 0)
             mix_chi(S, 2, 1)
-            for c in range(4):
-                first_product(0, 1, c)
-                times_chi(0, 1, c)
+            times_chi(0, 1, 0)
+            times_chi(0, 1, 1)
+            for half in range(2):
+                for c in (2, 3):
+                    first_product(0, half, c)
+            for half in range(2):
+                for c in (2, 3):
+                    times_chi(0, half, c)
+                keep_warm(t_bank(0, half, 3))
             for slab in range(1, SLABS):
                 if slab < 3:
                     quantize_chi(slab, 0)
@@ -319,14 +347,14 @@ def tile_fragment_lda_exchange_h3_kernel(tc, chi, dens, frag, core, wx, out_0, o
                     quantize_chi(3, 0)
                     quantize_chi(3, 1)
                 if slab == 3:
-                    times_chi(slab, 0, 0)
+                    quantize_y(0)
+                    store_codes(0)
                 for s in range(PACK):
                     quantize_h(slab - 1, s)
-                if slab < 3:
-                    times_chi(slab, 0, 0)
                 if slab == 1:
-                    times_chi(slab, 0, 1)
                     quantize_frag(1)
+                times_chi(slab, 0, 0)
+                if slab == 1:
                     mix_chi(GP, 3, 1)
                     mix_chi(GP, 3, 0)
                     widen_wx()
@@ -339,39 +367,40 @@ def tile_fragment_lda_exchange_h3_kernel(tc, chi, dens, frag, core, wx, out_0, o
                     first_product(slab, 0, 3)
                 for s in range(PACK):
                     second_product(slab - 1, s)
-                if slab == 1:
-                    times_chi(slab, 0, 2)
-                    times_chi(slab, 0, 3)
                 if slab == 2:
                     first_product(slab, 0, 3)
+                if slab < 3:
                     times_chi(slab, 0, 1)
                 for s in range(PACK):
                     add_core(slab - 1, s)
-                    log_rho(slab - 1, s, s + 1)
+                    log_rho(slab - 1, s)
                 for s in (3, 2, 1, 0):
                     power(slab - 1, s, s + 1)
-                if slab > 1:
-                    for c in range(4 - slab, 4):
-                        times_chi(slab, 0, c)
+                for c in range(2 if slab < 3 else 1, 4):
+                    times_chi(slab, 0, c)
                 for c in range(4):
                     first_product(slab, 1, c)
                 for c in range(4):
                     times_chi(slab, 1, c)
                     if slab == 2:
                         first_product(3, 0, c)
-            quantize_y(0)
-            store_codes(0)
+                    elif c % 2:
+                        keep_warm(t_bank(slab, 1, c))
             for s in range(PACK):
                 quantize_h(3, s)
                 second_product(3, s)
-            for s in (3, 2, 1, 0):
-                weigh(GP, 2, s)
-            store_y(2)
-            for s in range(PACK):
-                add_core(3, s)
-                log_rho(3, s, s + 1)
             quantize_y(1)
             store_codes(1)
+            for s in (3, 2, 1):
+                weigh(GP, 2, s)
+            for s in range(PACK - 1):
+                add_core(3, s)
+                log_rho(3, s)
+            for lo in (0, 256):
+                add_core(3, 3, lo, lo + 256)
+                log_rho(3, 3, lo, lo + 256)
+            weigh(V, 2, 0)
+            store_y(2)
             mix_y(V, 2)
             for lo in range(0, F, 128):
                 power(3, 0, PACK, lo, lo + 128)

from contextlib import ExitStack

import concourse.mybir as mybir
from concourse.masks import make_identity

B, G, F = 1024, 2048, 512
FLOPS = 2 * B * B * G + 2 * G * B * F

F32 = mybir.dt.float32
BF16 = mybir.dt.bfloat16
U32 = mybir.dt.uint32
I32 = mybir.dt.int32
U8 = mybir.dt.uint8
FP8X4 = mybir.dt.float8_e4m3fn_x4
ALU = mybir.AluOpType
ACT = mybir.ActivationFunctionType

P = 128
PACK = 4
SPAN = P * PACK
HALVES = B // SPAN
SLABS = G // SPAN


def tile_fragment_lda_exchange_h3_kernel(tc, chi, dens, frag, core, wx, out_0, out_1, out_2):
    nc = tc.nc
    V, S, GP = nc.vector, nc.scalar, nc.gpsimd
    with ExitStack() as ctx:
        sb = ctx.enter_context(tc.tile_pool(name="sb", bufs=1))
        ps = ctx.enter_context(tc.psum_pool(name="ps", bufs=1))

        def tiles(name, count, shape, dtype):
            return [sb.tile(shape, dtype, name="%s%d" % (name, i), align_bytes=64) for i in range(count)]

        banks = [ps.tile([P, SPAN], F32, name="bank%d" % i) for i in range(8)]
        t_banks, rho_banks = banks[:4], banks[4:]

        ident = sb.tile([P, P], F32, name="ident")
        warm = sb.tile([P, 8], F32, name="warm")
        dens_raw = tiles("dens_raw", 4, [P, 2, B], BF16)
        dens_words = tiles("dens_words", 4, [P, 2, HALVES, P, 2], F32)
        dens_codes = tiles("dens_codes", HALVES, [P, PACK, HALVES, P], U32)
        dens_scales = tiles("dens_scales", HALVES, [P, PACK, HALVES, P], U8)
        chi_raw = tiles("chi_raw", SLABS * HALVES, [P, PACK, SPAN], BF16)
        h_pairs = tiles("h_pairs", SLABS, [P, HALVES, SPAN * PACK], BF16)
        chi_shared = sb.tile([P, SPAN + SPAN // 2, PACK], BF16, name="chi_shared", align_bytes=64)
        own = tiles("chi_mixed", 4, [P, SPAN, PACK], BF16)
        chi_mixed = [chi_shared[:, SPAN // 2 :, :], own[0][:], own[1][:], chi_shared[:, :SPAN, :], own[2][:], own[3][:]]
        ones = sb.tile([P, SPAN], BF16, name="ones", align_bytes=64)
        ones_codes = sb.tile([P, P], U32, name="ones_codes", align_bytes=64)
        ones_scales = sb.tile([P, P], U8, name="ones_scales", align_bytes=64)
        frag_mixed = tiles("frag_mixed", HALVES, [P, F, PACK], BF16)
        chi_mixed += [h_pairs[0][:, 0, :].rearrange("p (c j) -> p c j", j=PACK), frag_mixed[1][:]]
        chi_codes = tiles("chi_codes", 2 * HALVES, [P, SPAN], U32)
        chi_scales = tiles("chi_scales", 2 * HALVES, [P, SPAN], U8)
        frag_raw = tiles("frag_raw", HALVES, [P, PACK, F], BF16)
        frag_codes = tiles("frag_codes", HALVES, [P, F], U32)
        frag_scales = tiles("frag_scales", HALVES, [P, F], U8)
        h_codes = sb.tile([P, HALVES * SPAN], U32, name="h_codes", align_bytes=64)
        h_scales = sb.tile([P, HALVES * SPAN], U8, name="h_scales", align_bytes=64)
        core_sb = tiles("core_sb", SLABS, [P, PACK, F], BF16)
        wx_sb = sb.tile([P, SLABS, PACK], BF16, name="wx_sb")
        wx_f32 = sb.tile([P, SLABS, PACK], F32, name="wx_f32")
        rho = 2 * tiles("rho", 2, [P, PACK, F], F32)
        y = [
            h_pairs[slab + 1][:].rearrange("p h c -> p (h c)").bitcast(F32).rearrange("p (s f) -> p s f", s=PACK)
            for slab in range(SLABS - 1)
        ] + [rho[3][:]]
        y_mixed = tiles("y_mixed", 2, [P, F, PACK], BF16)
        y_codes = tiles("y_codes", SLABS, [P, F], U32)
        y_scales = sb.tile([P, SLABS, F], U8, name="y_scales", align_bytes=64)

        def rows4(matrix, span):
            return matrix[span * SPAN : (span + 1) * SPAN, :].rearrange("(p j) w -> p j w", j=PACK)

        def copy_on(engine, out, in_):
            if engine is S:
                engine.copy(out=out, in_=in_)
            elif engine is V:
                engine.tensor_copy(out=out, in_=in_)
            else:
                engine.tensor_scalar(out=out, in0=in_, scalar1=1.0, scalar2=0.0, op0=ALU.mult, op1=ALU.add)

        def interleave(engine, mixed, raw, lo, hi):
            if engine is GP:
                copy_on(engine, mixed[:, lo:hi, :], raw[:, :, lo:hi].rearrange("p j c -> p c j"))
            else:
                copy_on(
                    engine,
                    mixed[:, lo:hi, :].rearrange("p (c i) j -> p c j i", i=4),
                    raw[:, :, lo:hi].rearrange("p j (c i) -> p c j i", i=4),
                )

        def quantize(codes, scales, values):
            nc.vector.quantize_mx(out=codes.bitcast(FP8X4), scales=scales, in_=values)

        def load_dens(half, pair):
            nc.sync.dma_start(out=dens_raw[2 * half + pair][:], in_=rows4(dens, half)[:, 2 * pair : 2 * pair + 2, :])

        def load_chi(slab, half, lo=0, hi=SPAN):
            nc.sync.dma_start(
                out=chi_raw[2 * slab + half][:, :, lo:hi],
                in_=rows4(chi, half)[:, :, slab * SPAN + lo : slab * SPAN + hi],
            )

        def load_frag(half):
            nc.sync.dma_start(out=frag_raw[half][:], in_=rows4(frag, half))

        def load_core(slab):
            nc.sync.dma_start(out=core_sb[slab][:], in_=rows4(core, slab))

        def load_wx():
            nc.sync.dma_start(out=wx_sb[:], in_=wx.rearrange("(g p s) -> p g s", p=P, s=PACK))

        def widen_wx():
            nc.scalar.copy(out=wx_f32[:], in_=wx_sb[:])

        def dens_bank(half, pair, tt):
            return banks[4 * (1 - half) + 2 * pair + tt][:].rearrange("p (k u m) -> p k u m", k=HALVES, u=2)

        def turn_dens(half, pair):
            words = dens_raw[2 * half + pair][:].bitcast(F32)
            for tt in range(2):
                for k in range(HALVES):
                    for u in range(2):
                        nc.tensor.transpose(
                            dens_bank(half, pair, tt)[:, k, u, :], words[:, tt, 256 * k + u : 256 * (k + 1) : 2], ident[:]
                        )

        def drain_dens(engine, half, pair, tt):
            copy_on(
                engine,
                dens_words[2 * half + pair][:, tt, :, :, :],
                dens_bank(half, pair, tt).rearrange("p k u m -> p k m u"),
            )

        def quantize_dens(half, pair):
            ts = slice(2 * pair, 2 * pair + 2)
            quantize(
                dens_codes[half][:, ts, :, :].rearrange("p t k m -> p (t k m)"),
                dens_scales[half][:, ts, :, :].rearrange("p t k m -> p (t k m)"),
                dens_words[2 * half + pair][:].rearrange("p t k m u -> p (t k m u)").bitcast(BF16),
            )

        def mix_chi(engine, slab, half, lo=0, hi=SPAN):
            interleave(engine, chi_mixed[2 * slab + half], chi_raw[2 * slab + half], lo, hi)

        def quantize_chi(slab, half, lo=0, hi=SPAN):
            i = 2 * (slab % 2) + half
            quantize(
                chi_codes[i][:, lo:hi],
                chi_scales[i][:, lo:hi],
                chi_mixed[2 * slab + half][:, lo:hi, :].rearrange("p c j -> p (c j)"),
            )

        def mix_frag(engine, half, lo=0, hi=F):
            interleave(engine, frag_mixed[half], frag_raw[half], lo, hi)

        def quantize_frag(half):
            quantize(frag_codes[half][:], frag_scales[half][:], frag_mixed[half][:].rearrange("p c j -> p (c j)"))

        def t_bank(slab, half, c):
            if slab == 0:
                return t_banks[2 * half + c % 2]
            return t_banks[c]

        def first_product(slab, half, c):
            cols = slice(c * P, (c + 1) * P)
            for t in range(PACK):
                for k in range(HALVES):
                    i = 2 * (slab % 2) + k
                    nc.tensor.matmul_mx(
                        out=t_bank(slab, half, c)[:, t * P : (t + 1) * P],
                        lhsT=dens_codes[half][:, t, k, :].bitcast(FP8X4),
                        lhsT_scale=dens_scales[half][:, t, k, :],
                        rhs=chi_codes[i][:, cols].bitcast(FP8X4),
                        rhs_scale=chi_scales[i][:, cols],
                        start=(k == 0),
                        stop=(k == HALVES - 1),
                    )

        def keep_warm(bank, passes=8):
            codes, scales = ones_codes, ones_scales
            for i in range(passes):
                nc.tensor.matmul_mx(
                    out=bank[:, :P],
                    lhsT=codes[:, :P].bitcast(FP8X4),
                    lhsT_scale=scales[:, :P],
                    rhs=codes[:, :P].bitcast(FP8X4),
                    rhs_scale=scales[:, :P],
                    start=True,
                    stop=True,
                )

        def times_chi(slab, half, c):
            nc.vector.tensor_tensor(
                out=h_pairs[slab][:].rearrange("p x (y h m t) -> p (x y) h m t", y=2, h=HALVES, t=PACK)[
                    :, :, half, 32 * c : 32 * (c + 1), :
                ],
                in0=t_bank(slab, half, c)[:].rearrange("p (t m s) -> p s m t", t=PACK, s=PACK),
                in1=chi_mixed[2 * slab + half][:, c * P : (c + 1) * P, :].rearrange("p (m s) t -> p s m t", s=PACK),
                op=ALU.mult,
            )

        def quantize_h(slab, s):
            lo, hi = s * HALVES * P, (s + 1) * HALVES * P
            quantize(
                h_codes[:, lo:hi], h_scales[:, lo:hi], h_pairs[slab][:].rearrange("p x c -> p (x c)")[:, PACK * lo : PACK * hi]
            )

        def rho_bank(slab, s):
            return rho_banks[(4 * slab + s) % 4]

        def second_product(slab, s):
            for half in range(HALVES):
                cols = slice((HALVES * s + half) * P, (HALVES * s + half + 1) * P)
                nc.tensor.matmul_mx(
                    out=rho_bank(slab, s)[:],
                    lhsT=h_codes[:, cols].bitcast(FP8X4),
                    lhsT_scale=h_scales[:, cols],
                    rhs=frag_codes[half][:].bitcast(FP8X4),
                    rhs_scale=frag_scales[half][:],
                    start=(half == 0),
                    stop=(half == HALVES - 1),
                )

        def add_core(slab, s, lo=0, hi=F):
            nc.vector.tensor_tensor(
                out=rho[slab][:, s, lo:hi], in0=rho_bank(slab, s)[:, lo:hi], in1=core_sb[slab][:, s, lo:hi], op=ALU.add
            )

        def log_rho(slab, s, lo=0, hi=F):
            nc.scalar.activation(out=rho[slab][:, s, lo:hi], in_=rho[slab][:, s, lo:hi], func=ACT.Ln)

        def power(slab, s0=0, s1=PACK, lo=0, hi=F):
            nc.scalar.activation(out=rho[slab][:, s0:s1, lo:hi], in_=rho[slab][:, s0:s1, lo:hi], func=ACT.Exp, scale=4.0 / 3.0)

        def weigh(engine, slab, s, lo=0, hi=F):
            piece, src, w = y[slab][:, s, lo:hi], rho[slab][:, s, lo:hi], wx_f32[:, slab, s : s + 1]
            if engine is S:
                engine.activation(out=piece, in_=src, func=ACT.Copy, scale=w)
            else:
                engine.tensor_scalar(out=piece, in0=src, scalar1=w, scalar2=0.0, op0=ALU.mult, op1=ALU.add)

        def mix_y(engine, slab, lo=0, hi=F):
            interleave(engine, y_mixed[slab % 2], y[slab], lo, hi)

        def quantize_y(slab, lo=0, hi=F):
            quantize(
                y_codes[slab][:, lo:hi],
                y_scales[:, slab, lo:hi],
                y_mixed[slab % 2][:, lo:hi, :].rearrange("p c j -> p (c j)"),
            )

        def store_y(slab, lo=0, hi=F, queue=nc.sync):
            queue.dma_start(out=rows4(out_0, slab)[:, :, lo:hi], in_=y[slab][:, :, lo:hi])

        def store_codes(slab, lo=0, hi=F, queue=nc.sync):
            queue.dma_start(
                out=out_1[slab, :, lo:hi, :].rearrange("p m t -> p (m t)").bitcast(I32),
                in_=y_codes[slab][:, lo:hi].bitcast(I32),
            )

        def store_scales(q, lo, hi, queue=nc.sync):
            queue.dma_start(
                out=out_2[lo:hi, 4 * q : 4 * q + 4, :].rearrange("g r m -> r g m").bitcast(I32),
                in_=y_scales[32 * q : 32 * q + 4, lo:hi, :].bitcast(I32),
            )

        with tc.manual_schedule():
            load_dens(0, 0)
            load_dens(0, 1)
            load_dens(1, 0)
            load_dens(1, 1)
            load_chi(0, 0, 0, 256)
            load_chi(0, 1, 0, 256)
            load_chi(0, 0, 256, 512)
            load_chi(0, 1, 256, 512)
            load_chi(1, 0)
            load_chi(1, 1)
            load_frag(0)
            load_frag(1)
            load_chi(2, 0)
            load_chi(3, 1)
            load_core(0)
            load_chi(2, 1)
            load_chi(3, 0)
            load_wx()
            load_core(1)
            load_core(2)
            load_core(3)
            V.memset(ones[:], 1.0)
            quantize(ones_codes[:], ones_scales[:], ones[:])
            keep_warm(banks[0], 16)
            make_identity(nc, ident[:])
            S.activation(out=warm[:], in_=ones[:, :8], func=ACT.Ln)
            for half in range(2):
                for pair in range(2):
                    if (half, pair) == (1, 0):
                        keep_warm(banks[3])
                    turn_dens(half, pair)
                    drain_dens(S, half, pair, 0)
                    drain_dens(V if (half, pair) == (0, 0) else S, half, pair, 1)
            quantize_dens(0, 0)
            quantize_dens(0, 1)
            keep_warm(banks[4])
            mix_chi(V, 0, 0, 0, 256)
            mix_chi(V, 0, 1, 0, 256)
            quantize_chi(0, 0, 0, 256)
            quantize_chi(0, 1, 0, 256)
            quantize_dens(1, 0)
            quantize_dens(1, 1)
            mix_chi(V, 0, 0, 256, 512)
            mix_chi(S, 0, 1, 256, 512)
            first_product(0, 0, 0)
            first_product(0, 0, 1)
            first_product(0, 1, 0)
            first_product(0, 1, 1)
            times_chi(0, 0, 0)
            quantize_chi(0, 0, 256, 512)
            quantize_chi(0, 1, 256, 512)
            times_chi(0, 0, 1)
            mix_chi(GP, 1, 1)
            mix_chi(S, 1, 0)
            mix_frag(S, 0)
            mix_frag(S, 1)
            mix_chi(S, 2, 0)
            mix_chi(S, 2, 1)
            times_chi(0, 1, 0)
            times_chi(0, 1, 1)
            for half in range(2):
                for c in (2, 3):
                    first_product(0, half, c)
            for half in range(2):
                for c in (2, 3):
                    times_chi(0, half, c)
                keep_warm(t_bank(0, half, 3))
            for slab in range(1, SLABS):
                if slab < 3:
                    quantize_chi(slab, 0)
                    quantize_chi(slab, 1)
                    for c in range(3):
                        first_product(slab, 0, c)
                if slab == 1:
                    quantize_frag(0)
                if slab == 2:
                    quantize_chi(3, 0)
                    quantize_chi(3, 1)
                if slab == 3:
                    quantize_y(0)
                    store_codes(0)
                for s in range(PACK):
                    quantize_h(slab - 1, s)
                if slab == 1:
                    quantize_frag(1)
                times_chi(slab, 0, 0)
                if slab == 1:
                    mix_chi(GP, 3, 1)
                    mix_chi(GP, 3, 0)
                    widen_wx()
                else:
                    for s in (3, 2, 1, 0):
                        weigh(GP, slab - 2, s)
                    store_y(slab - 2)
                    mix_y(GP, slab - 2)
                if slab == 1:
                    first_product(slab, 0, 3)
                for s in range(PACK):
                    second_product(slab - 1, s)
                if slab == 2:
                    first_product(slab, 0, 3)
                if slab < 3:
                    times_chi(slab, 0, 1)
                for s in range(PACK):
                    add_core(slab - 1, s)
                    log_rho(slab - 1, s)
                for s in (3, 2, 1, 0):
                    power(slab - 1, s, s + 1)
                for c in range(2 if slab < 3 else 1, 4):
                    times_chi(slab, 0, c)
                for c in range(4):
                    first_product(slab, 1, c)
                for c in range(4):
                    times_chi(slab, 1, c)
                    if slab == 2:
                        first_product(3, 0, c)
                    elif c % 2:
                        keep_warm(t_bank(slab, 1, c))
            for s in range(PACK):
                quantize_h(3, s)
                second_product(3, s)
            quantize_y(1)
            store_codes(1)
            for s in (3, 2, 1):
                weigh(GP, 2, s)
            for s in range(PACK - 1):
                add_core(3, s)
                log_rho(3, s)
            for lo in (0, 256):
                add_core(3, 3, lo, lo + 256)
                log_rho(3, 3, lo, lo + 256)
            weigh(V, 2, 0)
            store_y(2)
            mix_y(V, 2)
            for lo in range(0, F, 128):
                power(3, 0, PACK, lo, lo + 128)
            quantize_y(2)
            store_codes(2)
            for q in range(4):
                store_scales(q, 0, 3)
            for lo in range(0, F, 128):
                for s in range(PACK):
                    weigh(V, 3, s, lo, lo + 128)
                if lo % 256:
                    store_y(3, lo - 128, lo + 128)
                if lo == 128:
                    mix_y(V, 3, 0, 128)
                if lo == 256:
                    mix_y(V, 3, 128, 256)
                    mix_y(S, 3, 256, 384)
            quantize_y(3, 0, 256)
            store_codes(3, 0, 256, queue=S)
            mix_y(V, 3, 384, 512)
            quantize_y(3, 256, 512)
            store_codes(3, 256, 512, queue=S)
            for q in range(4):
                store_scales(q, 3, 4, S if q % 2 else nc.sync)
